import numpy as np
import ml_dtypes


def mxq(x, axis, fmt="e4m3"):
    dtype, down = {"e4m3": (ml_dtypes.float8_e4m3fn, 7), "e5m2": (ml_dtypes.float8_e5m2, 14)}[fmt]
    v = np.moveaxis(np.asarray(x, np.float32).astype(ml_dtypes.bfloat16).astype(np.float64), axis, -1)
    blocks = v.reshape(v.shape[:-1] + (-1, 32))
    amax = np.abs(blocks).max(-1, keepdims=True)
    byte = np.maximum(np.where(amax > 0, np.frexp(amax)[1] - 1 + 127, 0) - down, 1)
    scale = np.exp2(byte - 127.0)
    codes = (blocks / scale).astype(np.float32).astype(dtype).astype(np.float64)
    return np.moveaxis((codes * scale).reshape(v.shape), -1, axis)


WIDE = False


def mx_kscale(k):
    if not WIDE:
        return np.ones(k)
    levels = np.array([10, -10, 5, -5, 0])
    if k % 512:
        return np.exp2(np.random.permutation(np.resize(levels, k // 32))).repeat(32)
    a = np.empty((k // 512, 16))
    for p in range(k // 512):
        a[p, :8] = np.random.permutation(np.resize(levels, 8))
        for g in range(8):
            far = levels[np.abs(levels - a[p, g]) >= 10]
            a[p, g + 8] = far[np.random.randint(len(far))]
    return np.exp2(a.ravel()).repeat(32)


BF16 = ml_dtypes.bfloat16


def bf(x):
    return np.asarray(x, np.float32).astype(BF16)


def f64(x):
    return np.asarray(x).astype(np.float64)


E2M1 = np.array([0.0, 0.5, 1.0, 1.5, 2.0, 3.0, 4.0, 6.0, -0.0, -0.5, -1.0, -1.5, -2.0, -3.0, -4.0, -6.0])


def pack_weight(w, fmt):
    k, n = w.shape
    w = f64(bf(w)).reshape(k // 32, 32, n)
    amax = np.abs(w).max(1)
    if fmt == "e4m3":
        byte = np.frexp(amax)[1] - 1 + 127 - 7
    else:
        mant, ex = np.frexp(amax / 6.0)
        byte = np.where(mant > 0.5, ex, ex - 1) + 127
    byte = np.clip(np.where(amax > 0, byte, 1), 1, 254)
    scaled = (w * np.exp2(127.0 - byte)[:, None, :]).reshape(k, n).astype(np.float32)
    by_word = np.ascontiguousarray(scaled.reshape(k // 512, 128, 4, n).transpose(0, 1, 3, 2))
    if fmt == "e4m3":
        words = by_word.astype(ml_dtypes.float8_e4m3fn).view(np.uint8)
    else:
        c = by_word.astype(ml_dtypes.float4_e2m1fn).view(np.uint8) & 0xF
        words = c[..., 0::2] | (c[..., 1::2] << 4)
    return np.ascontiguousarray(words), np.ascontiguousarray(byte.astype(np.uint8).reshape(k // 512, 16, n))


def unpack_weight(words, scales, fmt):
    g, p, n, _ = words.shape
    if fmt == "e4m3":
        vals = np.ascontiguousarray(words).view(ml_dtypes.float8_e4m3fn).astype(np.float64)
    else:
        nib = np.empty((g, p, n, 4), np.uint8)
        nib[..., 0::2] = words & 0xF
        nib[..., 1::2] = words >> 4
        vals = E2M1[nib]
    vals = vals * np.repeat(np.exp2(scales.astype(np.float64) - 127.0), 8, axis=1)[..., None]
    return vals.transpose(0, 1, 3, 2).reshape(g * 512, n)
def pack4(w):
    words, scales = pack_weight(w, "e2m1")
    return words.reshape(words.shape[0], 128, -1), scales


def unpack4(words, scales):
    return unpack_weight(words.reshape(words.shape[0], 128, -1, 2), scales, "e2m1")


M, KA, KC, N = 2048, 512, 1024, 1024


def setup_inputs():
    s = mx_kscale(KA)
    u = mx_kscale(KC)
    mass = np.exp(0.3 * np.random.standard_normal((M, 1)))
    strength = np.exp(0.3 * np.random.standard_normal(N))
    major_path = np.random.standard_normal((M, KA)) ** 2 * mass
    minor_path = np.random.standard_normal((M, KC)) ** 2 * mass
    major_coef = 0.5 * np.random.standard_normal((KA, N)) ** 2 * strength / KA
    minor_coef = 0.5 * np.random.standard_normal((KC, N)) ** 2 * strength / KC
    minor_words, minor_scales = pack4(minor_coef / u[:, None])
    return {"major_path": bf(major_path * s),
            "major_coef": bf(major_coef / s[:, None]),
            "minor_path": bf(minor_path * u),
            "minor_words": minor_words,
            "minor_scales": minor_scales,
            "planck": bf(np.exp(0.3 * np.random.standard_normal((M, N)))),
            "emissivity": bf(np.random.uniform(0.6, 0.98, N))}


def reference(major_path, major_coef, minor_path, minor_words, minor_scales, planck, emissivity):
    major = mxq(f64(major_path), 1, "e4m3") @ mxq(f64(major_coef), 0, "e4m3")
    minor = mxq(f64(minor_path), 1, "e4m3") @ unpack4(minor_words, minor_scales)
    tau = major + minor
    return np.exp(-tau) * f64(planck) * f64(emissivity)

@@ -1,0 +1,228 @@
+from contextlib import ExitStack
+
+import concourse.mybir as mybir
+from concourse.masks import make_identity
+
+M, KA, KC, N = 2048, 512, 1024, 1024
+FLOPS = 2 * M * (KA + KC) * N
+
+F32 = mybir.dt.float32
+BF16 = mybir.dt.bfloat16
+I32 = mybir.dt.int32
+U32 = mybir.dt.uint32
+U8 = mybir.dt.uint8
+FP8X4 = mybir.dt.float8_e4m3fn_x4
+FP4X4 = mybir.dt.float4_e2m1fn_x4
+EXP = mybir.ActivationFunctionType.Exp
+MULT = mybir.AluOpType.mult
+
+P = 128
+PACK = 4
+K_PASS = P * PACK
+BANK = 512
+HALVES = N // BANK
+ROWS_PER_PART = 4
+PAIR = 2
+PAIRS = M // (P * PAIR)
+MINOR_PASSES = KC // K_PASS
+PASSES = MINOR_PASSES + 1
+MAJOR = MINOR_PASSES
+LOAD_GROUPS = [[0], [1], [2, 3], [4, 5], [6, 7]]
+
+
+def tile_longwave_surface_emission_s1_kernel(
+    tc, major_path, major_coef, minor_path, minor_words, minor_scales, planck, emissivity, out
+):
+    nc = tc.nc
+
+    def pair_rows(dram, first_pair, pairs):
+        width = dram.shape[1]
+        per_chunk = ROWS_PER_PART // PAIR
+        view = dram.rearrange("(c p j) w -> c p (j w)", p=P, j=ROWS_PER_PART)[first_pair // per_chunk]
+        start = (first_pair % per_chunk) * PAIR * width
+        return view[:, start : start + pairs * PAIR * width]
+
+    with ExitStack() as ctx:
+        keep = ctx.enter_context(tc.tile_pool(name="keep", bufs=1))
+        work = ctx.enter_context(tc.tile_pool(name="work", bufs=3))
+        psum = ctx.enter_context(tc.psum_pool(name="psum", bufs=1))
+        ctx.enter_context(tc.manual_schedule())
+
+        major_sb, minor_sb, planck_sb = {}, {}, {}
+
+        def load_rows(dram, group, into, label):
+            width = dram.shape[1]
+            tile = keep.tile([P, len(group) * PAIR * width], BF16, name="%s%d" % (label, group[0]), align_bytes=64)
+            nc.sync.dma_start(out=tile[:], in_=pair_rows(dram, group[0], len(group)))
+            for i, pair in enumerate(group):
+                into[pair] = tile[:, i * PAIR * width : (i + 1) * PAIR * width]
+
+        coef_raw = {}
+
+        def load_coef(half):
+            coef_raw[half] = keep.tile([P, PACK, BANK], BF16, name="coef_raw%d" % half, align_bytes=64)
+            rows = major_coef.rearrange("(p t) n -> p t n", t=PACK)
+            nc.sync.dma_start(out=coef_raw[half][:], in_=rows[:, :, half * BANK : (half + 1) * BANK])
+
+        ident = keep.tile([P, P], F32, name="ident")
+        make_identity(nc, ident[:])
+
+        minor_plane = keep.tile([P, MINOR_PASSES, N], U8, name="minor_plane", align_bytes=64)
+        nc.vector.memset(minor_plane[:].rearrange("p g n -> p (g n)").bitcast(I32), 0)
+        for quadrant in range(4):
+            nc.scalar.dma_start(
+                out=minor_plane[32 * quadrant : 32 * quadrant + 4, :, :].bitcast(I32),
+                in_=minor_scales[:, 4 * quadrant : 4 * quadrant + 4, :].rearrange("g r n -> r g n").bitcast(I32),
+            )
+
+        emis_sb = keep.tile([P, N // P], BF16, name="emis_sb")
+        minor_codes = keep.tile([P, MINOR_PASSES, 2 * N], U8, name="minor_codes", align_bytes=64)
+        nc.sync.dma_start(out=emis_sb[:], in_=emissivity.rearrange("(p c) -> p c", p=P))
+        load_coef(0)
+        load_rows(minor_path, LOAD_GROUPS[0], minor_sb, "minor")
+        load_rows(planck, LOAD_GROUPS[0], planck_sb, "planck")
+        load_rows(major_path, LOAD_GROUPS[0], major_sb, "major")
+        load_coef(1)
+        nc.sync.dma_start(out=minor_codes[:].bitcast(I32), in_=minor_words.rearrange("g p n -> p g n").bitcast(I32))
+        for group in LOAD_GROUPS[1:]:
+            load_rows(minor_path, group, minor_sb, "minor")
+            load_rows(major_path, group, major_sb, "major")
+            load_rows(planck, group, planck_sb, "planck")
+
+        emis_ps = psum.tile([P, BANK], F32, name="emis_ps")
+        emis_words = emis_sb[:].bitcast(F32)
+        per_part = emis_words.shape[1]
+        for c in range(per_part):
+            nc.tensor.transpose(
+                emis_ps[:, c:BANK:per_part], emis_words[:, c : c + 1].to_broadcast([P, P]), ident[:]
+            )
+        emis_row = emis_ps[:].bitcast(BF16)
+
+        coef_grouped, coef_codes, coef_plane = {}, {}, {}
+
+        def interleave_coef(half, copy):
+            coef_grouped[half] = keep.tile([P, BANK, PACK], BF16, name="coef_grouped%d" % half, align_bytes=64)
+            copy(
+                out=coef_grouped[half][:].rearrange("p (c i) t -> p c t i", i=4),
+                in_=coef_raw[half][:].rearrange("p t (c i) -> p c t i", i=4),
+            )
+
+        def quantize_coef(half):
+            coef_codes[half] = keep.tile([P, BANK], U32, name="coef_codes%d" % half, align_bytes=64)
+            coef_plane[half] = keep.tile([P, BANK], U8, name="coef_plane%d" % half, align_bytes=64)
+            nc.vector.quantize_mx(
+                out=coef_codes[half][:].bitcast(FP8X4),
+                scales=coef_plane[half][:],
+                in_=coef_grouped[half][:].rearrange("p c t -> p (c t)"),
+            )
+
+        turned, grouped, codes, planes, result, tau, trans = {}, {}, {}, {}, {}, {}, {}
+
+        def transpose_paths(pair):
+            for s in range(PASSES):
+                turned[s] = psum.tile([P, PAIR, 2, P], F32, name="turned%d" % s)
+                for j in range(PAIR):
+                    if s == MAJOR:
+                        words = major_sb[pair][:, j * KA : (j + 1) * KA].bitcast(F32)
+                    else:
+                        words = minor_sb[pair][:, j * KC + s * K_PASS : j * KC + (s + 1) * K_PASS].bitcast(F32)
+                    for u in range(2):
+                        nc.tensor.transpose(turned[s][:, j, u, :], words[:, u : K_PASS // 2 : 2], ident[:])
+
+        def copy_paths():
+            for s in range(PASSES):
+                grouped[s] = work.tile([P, PAIR * P * PACK], BF16, name="grouped%d" % s, bufs=2, align_bytes=64)
+                nc.scalar.copy(
+                    out=grouped[s][:].bitcast(F32).rearrange("p (j r u) -> p j r u", j=PAIR, u=2),
+                    in_=turned[s][:].rearrange("p j u r -> p j r u"),
+                )
+
+        def quantize_paths(pair):
+            for s in range(PASSES):
+                codes[pair, s] = work.tile([P, PAIR * P], U32, name="codes%d" % s, align_bytes=64)
+                planes[pair, s] = work.tile([P, PAIR * P], U8, name="planes%d" % s, align_bytes=64)
+                nc.vector.quantize_mx(
+                    out=codes[pair, s][:].bitcast(FP8X4), scales=planes[pair, s][:], in_=grouped[s][:]
+                )
+
+        def source(pair):
+            result[pair] = keep.tile([P, PAIR, N], F32, name="result%d" % pair)
+            for j in range(PAIR):
+                nc.vector.tensor_tensor(
+                    out=result[pair][:, j, :], in0=planck_sb[pair][:, j * N : (j + 1) * N], in1=emis_row, op=MULT
+                )
+
+        def multiply(pair, half):
+            cols = slice(half * BANK, (half + 1) * BANK)
+            for j in range(PAIR):
+                tau[half, j] = psum.tile([P, BANK], F32, name="tau%d%d" % (half, j))
+                rows = slice(j * P, (j + 1) * P)
+                for s in range(PASSES):
+                    if s == MAJOR:
+                        rhs, rhs_scale = coef_codes[half][:].bitcast(FP8X4), coef_plane[half][:]
+                    else:
+                        rhs = minor_codes[:, s, 2 * half * BANK : 2 * (half + 1) * BANK].bitcast(FP4X4)
+                        rhs_scale = minor_plane[:, s, cols]
+                    nc.tensor.matmul_mx(
+                        out=tau[half, j][:],
+                        lhsT=codes[pair, s][:, rows].bitcast(FP8X4),
+                        lhsT_scale=planes[pair, s][:, rows],
+                        rhs=rhs,
+                        rhs_scale=rhs_scale,
+                        start=(s == 0),
+                        stop=(s == PASSES - 1),
+                    )
+
+        def transmit(half, j):
+            if j == 0:
+                trans[half] = work.tile([P, PAIR, BANK], F32, name="trans")
+            nc.scalar.activation(out=trans[half][:, j, :], in_=tau[half, j][:], func=EXP, scale=-1.0)
+
+        def attenuate(pair, half, tiles):
+            part = result[pair][:, tiles, half * BANK : (half + 1) * BANK]
+            nc.vector.tensor_tensor(out=part, in0=part, in1=trans[half][:, tiles, :], op=MULT)
+
+        def store(pair, cols, tiles):
+            dst = pair_rows(out, pair, 1).rearrange("p (j n) -> p j n", j=PAIR)
+            nc.sync.dma_start(out=dst[:, tiles, cols], in_=result[pair][:, tiles, cols])
+
+        both = slice(0, PAIR)
+        whole = slice(0, N)
+
+        interleave_coef(0, nc.vector.tensor_copy)
+        transpose_paths(0)
+        copy_paths()
+        quantize_coef(0)
+        source(0)
+        quantize_paths(0)
+        interleave_coef(1, nc.scalar.copy)
+
+        for pair in range(PAIRS):
+            last = pair == PAIRS - 1
+            if not last:
+                transpose_paths(pair + 1)
+            if pair > 0:
+                transmit(1, 1)
+                attenuate(pair - 1, 1, both)
+                store(pair - 1, whole, both)
+            else:
+                quantize_coef(1)
+            if not last:
+                copy_paths()
+            multiply(pair, 0)
+            if not last:
+                quantize_paths(pair + 1)
+            transmit(0, 0)
+            transmit(0, 1)
+            multiply(pair, 1)
+            if not last:
+                source(pair + 1)
+            transmit(1, 0)
+            attenuate(pair, 0, both)
+
+        store(PAIRS - 1, slice(0, BANK), both)
+        attenuate(PAIRS - 1, 1, slice(0, 1))
+        store(PAIRS - 1, slice(BANK, N), slice(0, 1))
+        transmit(1, 1)
+        attenuate(PAIRS - 1, 1, slice(1, 2))
+        store(PAIRS - 1, slice(BANK, N), slice(1, 2))

@@ -27,7 +27,8 @@ PAIRS = M // (P * PAIR)
 MINOR_PASSES = KC // K_PASS
 PASSES = MINOR_PASSES + 1
 MAJOR = MINOR_PASSES
-LOAD_GROUPS = [[0], [1], [2, 3], [4, 5], [6, 7]]
+TAU_BANKS = 4
+FIRST_HALVED = 5
 
 
 def tile_longwave_surface_emission_s1_kernel(
@@ -67,6 +68,9 @@ def tile_longwave_surface_emission_s1_kernel(
         ident = keep.tile([P, P], F32, name="ident")
         make_identity(nc, ident[:])
 
+        emis_sb = keep.tile([P, N // P], BF16, name="emis_sb")
+        nc.scalar.dma_start(out=emis_sb[:], in_=emissivity.rearrange("(p c) -> p c", p=P))
+
         minor_plane = keep.tile([P, MINOR_PASSES, N], U8, name="minor_plane", align_bytes=64)
         nc.vector.memset(minor_plane[:].rearrange("p g n -> p (g n)").bitcast(I32), 0)
         for quadrant in range(4):
@@ -75,19 +79,35 @@ def tile_longwave_surface_emission_s1_kernel(
                 in_=minor_scales[:, 4 * quadrant : 4 * quadrant + 4, :].rearrange("g r n -> r g n").bitcast(I32),
             )
 
-        emis_sb = keep.tile([P, N // P], BF16, name="emis_sb")
-        minor_codes = keep.tile([P, MINOR_PASSES, 2 * N], U8, name="minor_codes", align_bytes=64)
-        nc.sync.dma_start(out=emis_sb[:], in_=emissivity.rearrange("(p c) -> p c", p=P))
-        load_coef(0)
-        load_rows(minor_path, LOAD_GROUPS[0], minor_sb, "minor")
-        load_rows(planck, LOAD_GROUPS[0], planck_sb, "planck")
-        load_rows(major_path, LOAD_GROUPS[0], major_sb, "major")
-        load_coef(1)
-        nc.sync.dma_start(out=minor_codes[:].bitcast(I32), in_=minor_words.rearrange("g p n -> p g n").bitcast(I32))
-        for group in LOAD_GROUPS[1:]:
+        minor_codes = {}
+
+        def load_words(half):
+            minor_codes[half] = keep.tile([P, MINOR_PASSES, 2 * BANK], U8, name="minor_codes%d" % half, align_bytes=64)
+            words = minor_words.rearrange("g p n -> p g n")[:, :, 2 * half * BANK : 2 * (half + 1) * BANK]
+            nc.sync.dma_start(out=minor_codes[half][:].bitcast(I32), in_=words.bitcast(I32))
+
+        def load_paths(group):
             load_rows(minor_path, group, minor_sb, "minor")
             load_rows(major_path, group, major_sb, "major")
+
+        def load_planck(group):
             load_rows(planck, group, planck_sb, "planck")
+
+        load_rows(minor_path, [0], minor_sb, "minor")
+        load_words(0)
+        load_rows(major_path, [0], major_sb, "major")
+        load_coef(0)
+        load_coef(1)
+        load_planck([0])
+        load_paths([1])
+        load_words(1)
+        load_paths([2])
+        load_planck([1])
+        load_planck([2, 3])
+        load_paths([3])
+        for group in ([4, 5], [6, 7]):
+            load_paths(group)
+            load_planck(group)
 
         emis_ps = psum.tile([P, BANK], F32, name="emis_ps")
         emis_words = emis_sb[:].bitcast(F32)
@@ -137,8 +157,8 @@ def tile_longwave_surface_emission_s1_kernel(
                     in_=turned[s][:].rearrange("p j u r -> p j r u"),
                 )
 
-        def quantize_paths(pair):
-            for s in range(PASSES):
+        def quantize_paths(pair, passes):
+            for s in passes:
                 codes[pair, s] = work.tile([P, PAIR * P], U32, name="codes%d" % s, align_bytes=64)
                 planes[pair, s] = work.tile([P, PAIR * P], U8, name="planes%d" % s, align_bytes=64)
                 nc.vector.quantize_mx(
@@ -146,83 +166,98 @@ def tile_longwave_surface_emission_s1_kernel(
                 )
 
         def source(pair):
-            result[pair] = keep.tile([P, PAIR, N], F32, name="result%d" % pair)
-            for j in range(PAIR):
+            result[pair] = keep.tile([P, PAIR * N], F32, name="result%d" % pair)
+            for j, start, stop in ((0, 0, BANK), (0, BANK, N), (1, 0, N)):
+                cols = slice(j * N + start, j * N + stop)
                 nc.vector.tensor_tensor(
-                    out=result[pair][:, j, :], in0=planck_sb[pair][:, j * N : (j + 1) * N], in1=emis_row, op=MULT
+                    out=result[pair][:, cols], in0=planck_sb[pair][:, cols], in1=emis_row[:, start:stop], op=MULT
                 )
 
         def multiply(pair, half):
             cols = slice(half * BANK, (half + 1) * BANK)
             for j in range(PAIR):
-                tau[half, j] = psum.tile([P, BANK], F32, name="tau%d%d" % (half, j))
+                tau[pair, half, j] = psum.tile([P, BANK], F32, name="tau%d" % (len(tau) % TAU_BANKS))
+            if half == 0:
+                order = [(j, s) for s in range(PASSES) for j in range(PAIR)]
+            else:
+                order = [(j, s) for j in range(PAIR) for s in range(PASSES)]
+            for j, s in order:
                 rows = slice(j * P, (j + 1) * P)
-                for s in range(PASSES):
-                    if s == MAJOR:
-                        rhs, rhs_scale = coef_codes[half][:].bitcast(FP8X4), coef_plane[half][:]
-                    else:
-                        rhs = minor_codes[:, s, 2 * half * BANK : 2 * (half + 1) * BANK].bitcast(FP4X4)
-                        rhs_scale = minor_plane[:, s, cols]
-                    nc.tensor.matmul_mx(
-                        out=tau[half, j][:],
-                        lhsT=codes[pair, s][:, rows].bitcast(FP8X4),
-                        lhsT_scale=planes[pair, s][:, rows],
-                        rhs=rhs,
-                        rhs_scale=rhs_scale,
-                        start=(s == 0),
-                        stop=(s == PASSES - 1),
-                    )
+                if s == MAJOR:
+                    rhs, rhs_scale = coef_codes[half][:].bitcast(FP8X4), coef_plane[half][:]
+                else:
+                    rhs, rhs_scale = minor_codes[half][:, s, :].bitcast(FP4X4), minor_plane[:, s, cols]
+                nc.tensor.matmul_mx(
+                    out=tau[pair, half, j][:],
+                    lhsT=codes[pair, s][:, rows].bitcast(FP8X4),
+                    lhsT_scale=planes[pair, s][:, rows],
+                    rhs=rhs,
+                    rhs_scale=rhs_scale,
+                    start=(s == 0),
+                    stop=(s == PASSES - 1),
+                )
 
-        def transmit(half, j):
-            if j == 0:
-                trans[half] = work.tile([P, PAIR, BANK], F32, name="trans")
-            nc.scalar.activation(out=trans[half][:, j, :], in_=tau[half, j][:], func=EXP, scale=-1.0)
+        def transmit(pair, half, j):
+            trans[pair, half, j] = work.tile([P, BANK], F32, name="trans%d%d" % (half, j), bufs=2)
+            nc.scalar.activation(out=trans[pair, half, j][:], in_=tau[pair, half, j][:], func=EXP, scale=-1.0)
 
-        def attenuate(pair, half, tiles):
-            part = result[pair][:, tiles, half * BANK : (half + 1) * BANK]
-            nc.vector.tensor_tensor(out=part, in0=part, in1=trans[half][:, tiles, :], op=MULT)
+        def attenuate(engine, pair, half, j):
+            part = result[pair][:, j * N + half * BANK : j * N + (half + 1) * BANK]
+            engine.tensor_tensor(out=part, in0=part, in1=trans[pair, half, j][:], op=MULT)
 
-        def store(pair, cols, tiles):
+        def store(pair, halves, tiles):
+            cols = slice(halves.start * BANK, halves.stop * BANK)
             dst = pair_rows(out, pair, 1).rearrange("p (j n) -> p j n", j=PAIR)
-            nc.sync.dma_start(out=dst[:, tiles, cols], in_=result[pair][:, tiles, cols])
+            src = result[pair][:].rearrange("p (j n) -> p j n", j=PAIR)
+            nc.sync.dma_start(out=dst[:, tiles, cols], in_=src[:, tiles, cols])
 
-        both = slice(0, PAIR)
-        whole = slice(0, N)
+        both, first, second = slice(0, 2), slice(0, 1), slice(1, 2)
+        last = PAIRS - 1
 
-        interleave_coef(0, nc.vector.tensor_copy)
         transpose_paths(0)
         copy_paths()
+        quantize_paths(0, range(MINOR_PASSES))
+        interleave_coef(0, nc.vector.tensor_copy)
+        quantize_paths(0, [MAJOR])
         quantize_coef(0)
-        source(0)
-        quantize_paths(0)
         interleave_coef(1, nc.scalar.copy)
 
-        for pair in range(PAIRS):
-            last = pair == PAIRS - 1
-            if not last:
-                transpose_paths(pair + 1)
-            if pair > 0:
-                transmit(1, 1)
-                attenuate(pair - 1, 1, both)
-                store(pair - 1, whole, both)
-            else:
-                quantize_coef(1)
-            if not last:
-                copy_paths()
-            multiply(pair, 0)
-            if not last:
-                quantize_paths(pair + 1)
-            transmit(0, 0)
-            transmit(0, 1)
-            multiply(pair, 1)
-            if not last:
-                source(pair + 1)
-            transmit(1, 0)
-            attenuate(pair, 0, both)
+        multiply(0, 0)
+        transpose_paths(1)
+        source(0)
+        quantize_coef(1)
+        copy_paths()
+        quantize_paths(1, range(PASSES))
+        for j in range(PAIR):
+            transmit(0, 0, j)
+            attenuate(nc.vector, 0, 0, j)
 
-        store(PAIRS - 1, slice(0, BANK), both)
-        attenuate(PAIRS - 1, 1, slice(0, 1))
-        store(PAIRS - 1, slice(BANK, N), slice(0, 1))
-        transmit(1, 1)
-        attenuate(PAIRS - 1, 1, slice(1, 2))
-        store(PAIRS - 1, slice(BANK, N), slice(1, 2))
+        for pair in range(1, PAIRS):
+            multiply(pair, 0)
+            if pair > 1:
+                transmit(pair - 2, 1, 1)
+                attenuate(nc.vector, pair - 2, 1, 1)
+                store(pair - 2, both if pair - 2 < FIRST_HALVED else second, both)
+            source(pair)
+            transmit(pair, 0, 0)
+            attenuate(nc.gpsimd, pair, 0, 0)
+            transmit(pair, 0, 1)
+            if pair < last:
+                transpose_paths(pair + 1)
+                copy_paths()
+                quantize_paths(pair + 1, range(PASSES))
+            attenuate(nc.vector, pair, 0, 1)
+            if pair >= FIRST_HALVED:
+                store(pair, first, both)
+            multiply(pair - 1, 1)
+            transmit(pair - 1, 1, 0)
+            attenuate(nc.vector, pair - 1, 1, 0)
+
+        multiply(last, 1)
+        transmit(last - 1, 1, 1)
+        attenuate(nc.vector, last - 1, 1, 1)
+        store(last - 1, second, both)
+        for j, tile in enumerate((first, second)):
+            transmit(last, 1, j)
+            attenuate(nc.vector, last, 1, j)
+            store(last, second, tile)

@@ -73,11 +73,6 @@ def tile_longwave_surface_emission_s1_kernel(
 
         minor_plane = keep.tile([P, MINOR_PASSES, N], U8, name="minor_plane", align_bytes=64)
         nc.vector.memset(minor_plane[:].rearrange("p g n -> p (g n)").bitcast(I32), 0)
-        for quadrant in range(4):
-            nc.scalar.dma_start(
-                out=minor_plane[32 * quadrant : 32 * quadrant + 4, :, :].bitcast(I32),
-                in_=minor_scales[:, 4 * quadrant : 4 * quadrant + 4, :].rearrange("g r n -> r g n").bitcast(I32),
-            )
 
         minor_codes = {}
 
@@ -94,6 +89,11 @@ def tile_longwave_surface_emission_s1_kernel(
             load_rows(planck, group, planck_sb, "planck")
 
         load_rows(minor_path, [0], minor_sb, "minor")
+        for quadrant in range(4):
+            nc.sync.dma_start(
+                out=minor_plane[32 * quadrant : 32 * quadrant + 4, :, :].bitcast(I32),
+                in_=minor_scales[:, 4 * quadrant : 4 * quadrant + 4, :].rearrange("g r n -> r g n").bitcast(I32),
+            )
         load_words(0)
         load_rows(major_path, [0], major_sb, "major")
         load_coef(0)
@@ -110,13 +110,13 @@ def tile_longwave_surface_emission_s1_kernel(
             load_planck(group)
 
         emis_ps = psum.tile([P, BANK], F32, name="emis_ps")
-        emis_words = emis_sb[:].bitcast(F32)
-        per_part = emis_words.shape[1]
-        for c in range(per_part):
-            nc.tensor.transpose(
-                emis_ps[:, c:BANK:per_part], emis_words[:, c : c + 1].to_broadcast([P, P]), ident[:]
-            )
         emis_row = emis_ps[:].bitcast(BF16)
+
+        def spread_emissivity():
+            words = emis_sb[:].bitcast(F32)
+            per_part = words.shape[1]
+            for c in range(per_part):
+                nc.tensor.transpose(emis_ps[:, c:BANK:per_part], words[:, c : c + 1].to_broadcast([P, P]), ident[:])
 
         coef_grouped, coef_codes, coef_plane = {}, {}, {}
 
@@ -138,16 +138,27 @@ def tile_longwave_surface_emission_s1_kernel(
 
         turned, grouped, codes, planes, result, tau, trans = {}, {}, {}, {}, {}, {}, {}
 
+        major_sorted = {}
+
+        def sort_major(pair):
+            major_sorted[pair] = work.tile([P, 2, PAIR * P], F32, name="major_sorted", bufs=2)
+            nc.scalar.copy(
+                out=major_sorted[pair][:], in_=major_sb[pair].bitcast(F32).rearrange("p (w u) -> p u w", u=2)
+            )
+
         def transpose_paths(pair):
             for s in range(PASSES):
                 turned[s] = psum.tile([P, PAIR, 2, P], F32, name="turned%d" % s)
                 for j in range(PAIR):
-                    if s == MAJOR:
-                        words = major_sb[pair][:, j * KA : (j + 1) * KA].bitcast(F32)
-                    else:
-                        words = minor_sb[pair][:, j * KC + s * K_PASS : j * KC + (s + 1) * K_PASS].bitcast(F32)
                     for u in range(2):
-                        nc.tensor.transpose(turned[s][:, j, u, :], words[:, u : K_PASS // 2 : 2], ident[:])
+                        if s != MAJOR:
+                            first_k = j * KC + s * K_PASS
+                            words = minor_sb[pair][:, first_k : first_k + K_PASS].bitcast(F32)[:, u::2]
+                        elif pair in major_sorted:
+                            words = major_sorted[pair][:, u, j * P : (j + 1) * P]
+                        else:
+                            words = major_sb[pair][:, j * KA : (j + 1) * KA].bitcast(F32)[:, u::2]
+                        nc.tensor.transpose(turned[s][:, j, u, :], words, ident[:])
 
         def copy_paths():
             for s in range(PASSES):
@@ -215,6 +226,7 @@ def tile_longwave_surface_emission_s1_kernel(
         last = PAIRS - 1
 
         transpose_paths(0)
+        spread_emissivity()
         copy_paths()
         quantize_paths(0, range(MINOR_PASSES))
         interleave_coef(0, nc.vector.tensor_copy)
@@ -232,20 +244,20 @@ def tile_longwave_surface_emission_s1_kernel(
             transmit(0, 0, j)
             attenuate(nc.vector, 0, 0, j)
 
-        for pair in range(1, PAIRS):
+        for pair in range(1, last):
             multiply(pair, 0)
             if pair > 1:
                 transmit(pair - 2, 1, 1)
                 attenuate(nc.vector, pair - 2, 1, 1)
-                store(pair - 2, both if pair - 2 < FIRST_HALVED else second, both)
+                store(pair - 2, both, both)
+            sort_major(pair + 1)
             source(pair)
             transmit(pair, 0, 0)
             attenuate(nc.gpsimd, pair, 0, 0)
             transmit(pair, 0, 1)
-            if pair < last:
-                transpose_paths(pair + 1)
-                copy_paths()
-                quantize_paths(pair + 1, range(PASSES))
+            transpose_paths(pair + 1)
+            copy_paths()
+            quantize_paths(pair + 1, range(PASSES))
             attenuate(nc.vector, pair, 0, 1)
             if pair >= FIRST_HALVED:
                 store(pair, first, both)
@@ -253,11 +265,18 @@ def tile_longwave_surface_emission_s1_kernel(
             transmit(pair - 1, 1, 0)
             attenuate(nc.vector, pair - 1, 1, 0)
 
-        multiply(last, 1)
-        transmit(last - 1, 1, 1)
-        attenuate(nc.vector, last - 1, 1, 1)
-        store(last - 1, second, both)
-        for j, tile in enumerate((first, second)):
-            transmit(last, 1, j)
-            attenuate(nc.vector, last, 1, j)
-            store(last, second, tile)
+        multiply(last, 0)
+        transmit(last - 2, 1, 1)
+        attenuate(nc.vector, last - 2, 1, 1)
+        store(last - 2, second, both)
+        source(last)
+        for j, (engine, tile) in enumerate(((nc.gpsimd, first), (nc.vector, second))):
+            transmit(last, 0, j)
+            attenuate(engine, last, 0, j)
+            store(last, first, tile)
+        for pair in (last - 1, last):
+            multiply(pair, 1)
+            for j, tile in enumerate((first, second)):
+                transmit(pair, 1, j)
+                attenuate(nc.vector, pair, 1, j)
+                store(pair, second, tile)

from contextlib import ExitStack

import concourse.mybir as mybir
from concourse.masks import make_identity

M, KA, KC, N = 2048, 512, 1024, 1024
FLOPS = 2 * M * (KA + KC) * N

F32 = mybir.dt.float32
BF16 = mybir.dt.bfloat16
I32 = mybir.dt.int32
U32 = mybir.dt.uint32
U8 = mybir.dt.uint8
FP8X4 = mybir.dt.float8_e4m3fn_x4
FP4X4 = mybir.dt.float4_e2m1fn_x4
EXP = mybir.ActivationFunctionType.Exp
MULT = mybir.AluOpType.mult

P = 128
PACK = 4
K_PASS = P * PACK
BANK = 512
HALVES = N // BANK
ROWS_PER_PART = 4
PAIR = 2
PAIRS = M // (P * PAIR)
MINOR_PASSES = KC // K_PASS
PASSES = MINOR_PASSES + 1
MAJOR = MINOR_PASSES
TAU_BANKS = 4
FIRST_HALVED = 5


def tile_longwave_surface_emission_s1_kernel(
    tc, major_path, major_coef, minor_path, minor_words, minor_scales, planck, emissivity, out
):
    nc = tc.nc

    def pair_rows(dram, first_pair, pairs):
        width = dram.shape[1]
        per_chunk = ROWS_PER_PART // PAIR
        view = dram.rearrange("(c p j) w -> c p (j w)", p=P, j=ROWS_PER_PART)[first_pair // per_chunk]
        start = (first_pair % per_chunk) * PAIR * width
        return view[:, start : start + pairs * PAIR * width]

    with ExitStack() as ctx:
        keep = ctx.enter_context(tc.tile_pool(name="keep", bufs=1))
        work = ctx.enter_context(tc.tile_pool(name="work", bufs=3))
        psum = ctx.enter_context(tc.psum_pool(name="psum", bufs=1))
        ctx.enter_context(tc.manual_schedule())

        major_sb, minor_sb, planck_sb = {}, {}, {}

        def load_rows(dram, group, into, label):
            width = dram.shape[1]
            tile = keep.tile([P, len(group) * PAIR * width], BF16, name="%s%d" % (label, group[0]), align_bytes=64)
            nc.sync.dma_start(out=tile[:], in_=pair_rows(dram, group[0], len(group)))
            for i, pair in enumerate(group):
                into[pair] = tile[:, i * PAIR * width : (i + 1) * PAIR * width]

        coef_raw = {}

        def load_coef(half):
            coef_raw[half] = keep.tile([P, PACK, BANK], BF16, name="coef_raw%d" % half, align_bytes=64)
            rows = major_coef.rearrange("(p t) n -> p t n", t=PACK)
            nc.sync.dma_start(out=coef_raw[half][:], in_=rows[:, :, half * BANK : (half + 1) * BANK])

        ident = keep.tile([P, P], F32, name="ident")
        make_identity(nc, ident[:])

        emis_sb = keep.tile([P, N // P], BF16, name="emis_sb")
        nc.scalar.dma_start(out=emis_sb[:], in_=emissivity.rearrange("(p c) -> p c", p=P))

        minor_plane = keep.tile([P, MINOR_PASSES, N], U8, name="minor_plane", align_bytes=64)
        nc.vector.memset(minor_plane[:].rearrange("p g n -> p (g n)").bitcast(I32), 0)

        minor_codes = {}

        def load_words(half):
            minor_codes[half] = keep.tile([P, MINOR_PASSES, 2 * BANK], U8, name="minor_codes%d" % half, align_bytes=64)
            words = minor_words.rearrange("g p n -> p g n")[:, :, 2 * half * BANK : 2 * (half + 1) * BANK]
            nc.sync.dma_start(out=minor_codes[half][:].bitcast(I32), in_=words.bitcast(I32))

        def load_paths(group):
            load_rows(minor_path, group, minor_sb, "minor")
            load_rows(major_path, group, major_sb, "major")

        def load_planck(group):
            load_rows(planck, group, planck_sb, "planck")

        load_rows(minor_path, [0], minor_sb, "minor")
        for quadrant in range(4):
            nc.sync.dma_start(
                out=minor_plane[32 * quadrant : 32 * quadrant + 4, :, :].bitcast(I32),
                in_=minor_scales[:, 4 * quadrant : 4 * quadrant + 4, :].rearrange("g r n -> r g n").bitcast(I32),
            )
        load_words(0)
        load_rows(major_path, [0], major_sb, "major")
        load_coef(0)
        load_coef(1)
        load_planck([0])
        load_paths([1])
        load_words(1)
        load_paths([2])
        load_planck([1])
        load_planck([2, 3])
        load_paths([3])
        for group in ([4, 5], [6, 7]):
            load_paths(group)
            load_planck(group)

        emis_ps = psum.tile([P, BANK], F32, name="emis_ps")
        emis_row = emis_ps[:].bitcast(BF16)

        def spread_emissivity():
            words = emis_sb[:].bitcast(F32)
            per_part = words.shape[1]
            for c in range(per_part):
                nc.tensor.transpose(emis_ps[:, c:BANK:per_part], words[:, c : c + 1].to_broadcast([P, P]), ident[:])

        coef_grouped, coef_codes, coef_plane = {}, {}, {}

        def interleave_coef(half, copy):
            coef_grouped[half] = keep.tile([P, BANK, PACK], BF16, name="coef_grouped%d" % half, align_bytes=64)
            copy(
                out=coef_grouped[half][:].rearrange("p (c i) t -> p c t i", i=4),
                in_=coef_raw[half][:].rearrange("p t (c i) -> p c t i", i=4),
            )

        def quantize_coef(half):
            coef_codes[half] = keep.tile([P, BANK], U32, name="coef_codes%d" % half, align_bytes=64)
            coef_plane[half] = keep.tile([P, BANK], U8, name="coef_plane%d" % half, align_bytes=64)
            nc.vector.quantize_mx(
                out=coef_codes[half][:].bitcast(FP8X4),
                scales=coef_plane[half][:],
                in_=coef_grouped[half][:].rearrange("p c t -> p (c t)"),
            )

        turned, grouped, codes, planes, result, tau, trans = {}, {}, {}, {}, {}, {}, {}

        major_sorted = {}

        def sort_major(pair):
            major_sorted[pair] = work.tile([P, 2, PAIR * P], F32, name="major_sorted", bufs=2)
            nc.scalar.copy(
                out=major_sorted[pair][:], in_=major_sb[pair].bitcast(F32).rearrange("p (w u) -> p u w", u=2)
            )

        def transpose_paths(pair):
            for s in range(PASSES):
                turned[s] = psum.tile([P, PAIR, 2, P], F32, name="turned%d" % s)
                for j in range(PAIR):
                    for u in range(2):
                        if s != MAJOR:
                            first_k = j * KC + s * K_PASS
                            words = minor_sb[pair][:, first_k : first_k + K_PASS].bitcast(F32)[:, u::2]
                        elif pair in major_sorted:
                            words = major_sorted[pair][:, u, j * P : (j + 1) * P]
                        else:
                            words = major_sb[pair][:, j * KA : (j + 1) * KA].bitcast(F32)[:, u::2]
                        nc.tensor.transpose(turned[s][:, j, u, :], words, ident[:])

        def copy_paths():
            for s in range(PASSES):
                grouped[s] = work.tile([P, PAIR * P * PACK], BF16, name="grouped%d" % s, bufs=2, align_bytes=64)
                nc.scalar.copy(
                    out=grouped[s][:].bitcast(F32).rearrange("p (j r u) -> p j r u", j=PAIR, u=2),
                    in_=turned[s][:].rearrange("p j u r -> p j r u"),
                )

        def quantize_paths(pair, passes):
            for s in passes:
                codes[pair, s] = work.tile([P, PAIR * P], U32, name="codes%d" % s, align_bytes=64)
                planes[pair, s] = work.tile([P, PAIR * P], U8, name="planes%d" % s, align_bytes=64)
                nc.vector.quantize_mx(
                    out=codes[pair, s][:].bitcast(FP8X4), scales=planes[pair, s][:], in_=grouped[s][:]
                )

        def source(pair):
            result[pair] = keep.tile([P, PAIR * N], F32, name="result%d" % pair)
            for j, start, stop in ((0, 0, BANK), (0, BANK, N), (1, 0, N)):
                cols = slice(j * N + start, j * N + stop)
                nc.vector.tensor_tensor(
                    out=result[pair][:, cols], in0=planck_sb[pair][:, cols], in1=emis_row[:, start:stop], op=MULT
                )

        def multiply(pair, half):
            cols = slice(half * BANK, (half + 1) * BANK)
            for j in range(PAIR):
                tau[pair, half, j] = psum.tile([P, BANK], F32, name="tau%d" % (len(tau) % TAU_BANKS))
            if half == 0:
                order = [(j, s) for s in range(PASSES) for j in range(PAIR)]
            else:
                order = [(j, s) for j in range(PAIR) for s in range(PASSES)]
            for j, s in order:
                rows = slice(j * P, (j + 1) * P)
                if s == MAJOR:
                    rhs, rhs_scale = coef_codes[half][:].bitcast(FP8X4), coef_plane[half][:]
                else:
                    rhs, rhs_scale = minor_codes[half][:, s, :].bitcast(FP4X4), minor_plane[:, s, cols]
                nc.tensor.matmul_mx(
                    out=tau[pair, half, j][:],
                    lhsT=codes[pair, s][:, rows].bitcast(FP8X4),
                    lhsT_scale=planes[pair, s][:, rows],
                    rhs=rhs,
                    rhs_scale=rhs_scale,
                    start=(s == 0),
                    stop=(s == PASSES - 1),
                )

        def transmit(pair, half, j):
            trans[pair, half, j] = work.tile([P, BANK], F32, name="trans%d%d" % (half, j), bufs=2)
            nc.scalar.activation(out=trans[pair, half, j][:], in_=tau[pair, half, j][:], func=EXP, scale=-1.0)

        def attenuate(engine, pair, half, j):
            part = result[pair][:, j * N + half * BANK : j * N + (half + 1) * BANK]
            engine.tensor_tensor(out=part, in0=part, in1=trans[pair, half, j][:], op=MULT)

        def store(pair, halves, tiles):
            cols = slice(halves.start * BANK, halves.stop * BANK)
            dst = pair_rows(out, pair, 1).rearrange("p (j n) -> p j n", j=PAIR)
            src = result[pair][:].rearrange("p (j n) -> p j n", j=PAIR)
            nc.sync.dma_start(out=dst[:, tiles, cols], in_=src[:, tiles, cols])

        both, first, second = slice(0, 2), slice(0, 1), slice(1, 2)
        last = PAIRS - 1

        transpose_paths(0)
        spread_emissivity()
        copy_paths()
        quantize_paths(0, range(MINOR_PASSES))
        interleave_coef(0, nc.vector.tensor_copy)
        quantize_paths(0, [MAJOR])
        quantize_coef(0)
        interleave_coef(1, nc.scalar.copy)

        multiply(0, 0)
        transpose_paths(1)
        source(0)
        quantize_coef(1)
        copy_paths()
        quantize_paths(1, range(PASSES))
        for j in range(PAIR):
            transmit(0, 0, j)
            attenuate(nc.vector, 0, 0, j)

        for pair in range(1, last):
            multiply(pair, 0)
            if pair > 1:
                transmit(pair - 2, 1, 1)
                attenuate(nc.vector, pair - 2, 1, 1)
                store(pair - 2, both, both)
            sort_major(pair + 1)
            source(pair)
            transmit(pair, 0, 0)
            attenuate(nc.gpsimd, pair, 0, 0)
            transmit(pair, 0, 1)
            transpose_paths(pair + 1)
            copy_paths()
            quantize_paths(pair + 1, range(PASSES))
            attenuate(nc.vector, pair, 0, 1)
            if pair >= FIRST_HALVED:
                store(pair, first, both)
            multiply(pair - 1, 1)
            transmit(pair - 1, 1, 0)
            attenuate(nc.vector, pair - 1, 1, 0)

        multiply(last, 0)
        transmit(last - 2, 1, 1)
        attenuate(nc.vector, last - 2, 1, 1)
        store(last - 2, second, both)
        source(last)
        for j, (engine, tile) in enumerate(((nc.gpsimd, first), (nc.vector, second))):
            transmit(last, 0, j)
            attenuate(engine, last, 0, j)
            store(last, first, tile)
        for pair in (last - 1, last):
            multiply(pair, 1)
            for j, tile in enumerate((first, second)):
                transmit(pair, 1, j)
                attenuate(nc.vector, pair, 1, j)
                store(pair, second, tile)
